import numpy as np
import ml_dtypes


def mxq(x, axis, fmt="e4m3"):
    dtype, down = {"e4m3": (ml_dtypes.float8_e4m3fn, 7), "e5m2": (ml_dtypes.float8_e5m2, 14)}[fmt]
    v = np.moveaxis(np.asarray(x, np.float32).astype(ml_dtypes.bfloat16).astype(np.float64), axis, -1)
    blocks = v.reshape(v.shape[:-1] + (-1, 32))
    amax = np.abs(blocks).max(-1, keepdims=True)
    byte = np.maximum(np.where(amax > 0, np.frexp(amax)[1] - 1 + 127, 0) - down, 1)
    scale = np.exp2(byte - 127.0)
    codes = (blocks / scale).astype(np.float32).astype(dtype).astype(np.float64)
    return np.moveaxis((codes * scale).reshape(v.shape), -1, axis)


WIDE = False


def mx_kscale(k):
    if not WIDE:
        return np.ones(k)
    levels = np.array([10, -10, 5, -5, 0])
    if k % 512:
        return np.exp2(np.random.permutation(np.resize(levels, k // 32))).repeat(32)
    a = np.empty((k // 512, 16))
    for p in range(k // 512):
        a[p, :8] = np.random.permutation(np.resize(levels, 8))
        for g in range(8):
            far = levels[np.abs(levels - a[p, g]) >= 10]
            a[p, g + 8] = far[np.random.randint(len(far))]
    return np.exp2(a.ravel()).repeat(32)


def f64(x):
    return np.asarray(x).astype(np.float64)


def striped(idx):
    return np.tile(idx.reshape(-1, 16).T, (8, 1)).astype(np.uint16)


def unstriped(offs):
    return offs[:16].T.reshape(-1).astype(np.int64)


def striped8(idx):
    return np.concatenate([x.reshape(-1, 16).T for x in idx]).astype(np.uint16)


def runs(offs, k):
    lists = np.stack([offs[16 * r : 16 * r + 16].T.reshape(-1) for r in range(8)]).astype(np.int64)
    return lists[np.arange(k) % 512 // 64]


def pack_weight(w):
    k, n = w.shape
    w = f64(np.asarray(w, np.float32).astype(ml_dtypes.bfloat16)).reshape(k // 32, 32, n)
    amax = np.abs(w).max(1)
    byte = np.clip(np.where(amax > 0, np.frexp(amax)[1] - 1 + 127 - 7, 1), 1, 254)
    scaled = (w * np.exp2(127.0 - byte)[:, None, :]).reshape(k, n).astype(np.float32)
    words = np.ascontiguousarray(scaled.reshape(k // 512, 128, 4, n).transpose(0, 1, 3, 2)).astype(ml_dtypes.float8_e4m3fn).view(np.uint8)
    return words, np.ascontiguousarray(byte.astype(np.uint8).reshape(k // 512, 16, n))


def unpack_weight(words, scales):
    g, p, n, _ = words.shape
    vals = np.ascontiguousarray(words).view(ml_dtypes.float8_e4m3fn).astype(np.float64) * np.repeat(np.exp2(scales.astype(np.float64) - 127.0), 8, axis=1)[..., None]
    return vals.transpose(0, 1, 3, 2).reshape(g * 512, n)


K, T, S, H, C, W = 512, 2048, 512, 512, 512, 256


def setup_inputs():
    n = np.random.standard_normal
    s = mx_kscale(K)[:, None]
    packed_xT = pack_weight(n((K, T)) * s)
    perm = np.stack([np.random.permutation(S) for _ in range(8)])
    return {
        "x_words": packed_xT[0],
        "x_scales": packed_xT[1],
        "w1": (n((K, H)) / np.sqrt(K) / s).astype(np.float32),
        "w2": (n((K, H)) / np.sqrt(K) / s).astype(np.float32),
        "gs": (np.random.uniform(0.5, 1.5, (K, 1)) / s).astype(np.float32),
        "offs": striped(np.random.permutation(T)[:S]),
        "two": striped(np.random.permutation(T)[:S]),
        "n1": striped8(np.stack([np.random.permutation(S) for _ in range(8)])),
        "n2": striped8(np.stack([np.random.permutation(S) for _ in range(8)])),
        "n3": striped8(np.stack([np.random.permutation(S) for _ in range(8)])),
        "cand": striped(np.random.permutation(T)[:C]),
        "n4": striped8(perm[:, :W]),
        "n5": striped8(perm[:, W:]),
    }


def reference(x_words, x_scales, w1, w2, gs, offs, two, n1, n2, n3, cand, n4, n5):
    x_cand = unpack_weight(x_words, x_scales)[:, unstriped(cand)]
    xq = unpack_weight(x_words, x_scales)[:, unstriped(offs)]
    y = mxq(f64(w1), 0, "e4m3").T @ xq
    x_two = unpack_weight(x_words, x_scales)[:, unstriped(two)]
    d = mxq(f64(w2), 0, "e4m3").T @ x_two
    z = f64(gs) * (np.maximum(np.minimum(y - (0.5 * (y[np.arange(H)[:, None], runs(n1, H)])), d[np.arange(H)[:, None], runs(n2, H)]), d[np.arange(H)[:, None], runs(n3, H)]))
    s = 0.0625 * ((x_cand.T @ mxq(z, 0, "e4m3")))
    pa = s[np.arange(C)[:, None], runs(n4, C)]
    pb = s[np.arange(C)[:, None], runs(n5, C)]
    rb = np.maximum(0.5 * pa, pb)
    ra = pb - pa
    ds = np.zeros((C, S))
    ds[np.arange(C)[:, None], runs(n4, C)] = ra
    out = ds.copy()
    out[np.arange(C)[:, None], runs(n5, C)] = rb
    return out

@@ -1,0 +1,171 @@
+from contextlib import ExitStack
+
+import concourse.mybir as mybir
+
+F32 = mybir.dt.float32
+BF16 = mybir.dt.bfloat16
+I32 = mybir.dt.int32
+U32 = mybir.dt.uint32
+U16 = mybir.dt.uint16
+U8 = mybir.dt.uint8
+FP8X4 = mybir.dt.float8_e4m3fn_x4
+ALU = mybir.AluOpType
+ACT = mybir.ActivationFunctionType
+
+P = 128
+PACK = 4
+T = 2048
+S = 512
+PAIRS = 256
+HALF = 256
+CHUNKS = ((0, 256), (256, 128), (384, 128))
+
+FLOPS = 3 * 2 * 512 * 512 * 512
+
+
+def tile_picked_twcclampblift_none_p_kernel(tc, x_words, x_scales, w1, w2, gs, offs, two, n1, n2, n3, cand, n4, n5, out):
+    nc = tc.nc
+    with ExitStack() as ctx:
+        lists = ctx.enter_context(tc.tile_pool(name="lists", bufs=1))
+        keep = ctx.enter_context(tc.tile_pool(name="keep", bufs=1))
+        psum = ctx.enter_context(tc.psum_pool(name="psum", bufs=1))
+
+        def load_list(dram, name):
+            tile = lists.tile(list(dram.shape), U16, name=name)
+            nc.sync.dma_start(tile[:], dram)
+            return tile
+
+        def load_weight(w, name):
+            halves = []
+            rows = w.rearrange("(p j) c -> p j c", j=PACK)
+            for h in range(2):
+                raw = keep.tile([P, PACK, HALF], F32, name="%s_raw%d" % (name, h))
+                nc.sync.dma_start(raw[:], rows[:, :, h * HALF:(h + 1) * HALF])
+                halves.append(raw)
+            return halves
+
+        offs_t = load_list(offs, "offs")
+        two_t = load_list(two, "two")
+        cand_t = load_list(cand, "cand")
+        gs_t = keep.tile([P, PACK], F32, name="gs_t")
+        nc.sync.dma_start(gs_t[:], gs.rearrange("(p t) o -> p (t o)", t=PACK))
+
+        table_s = keep.tile([P, T], U8, name="table_s", align_bytes=64)
+        nc.vector.memset(table_s[:].bitcast(I32), 0)
+        for q in range(4):
+            nc.sync.dma_start(table_s[32 * q:32 * q + 4, :].bitcast(I32), x_scales[0, 4 * q:4 * q + 4, :].bitcast(I32))
+
+        w1_raw = load_weight(w1, "w1")
+        table_w = keep.tile([P, T], U32, name="table_w", align_bytes=64)
+        nc.sync.dma_start(table_w[:].bitcast(I32), x_words[0].rearrange("p n t -> p (n t)").bitcast(I32))
+        w2_raw = load_weight(w2, "w2")
+        n1_t = load_list(n1, "n1")
+        n2_t = load_list(n2, "n2")
+        n3_t = load_list(n3, "n3")
+        n4_t = load_list(n4, "n4")
+        n5_t = load_list(n5, "n5")
+
+        twice = keep.tile([P, PACK], F32, name="twice")
+        sign32 = keep.tile([P, PACK], F32, name="sign32")
+        sign = keep.tile([P, PACK], BF16, name="sign")
+        size = keep.tile([P, PACK], F32, name="size")
+        nc.gpsimd.tensor_scalar(twice[:], gs_t[:], 0.0, 2.0, ALU.is_ge, ALU.mult)
+        nc.gpsimd.tensor_scalar(sign32[:], twice[:], 1.0, -1.0, ALU.mult, ALU.add)
+        nc.gpsimd.tensor_tensor(size[:], gs_t[:], sign32[:], ALU.mult)
+        nc.gpsimd.tensor_copy(sign[:], sign32[:])
+
+        def picked(table, dtype, offsets, name, dealt):
+            tile = keep.tile([P, S], dtype, name=name, align_bytes=64)
+            target = tile[:].rearrange("p (t m) -> p m t", t=PACK) if dealt else tile[:]
+            nc.vector.tensor_copy(target, table[:].indirect(offsets[:]))
+            return tile
+
+        def round_weight(halves, name):
+            grouped = keep.tile([P, PACK * S], BF16, name=name, align_bytes=64)
+            view = grouped[:].rearrange("p (t m j) -> p m j t", t=PACK, j=PACK)
+            for h in range(2):
+                m_half = HALF // PACK
+                nc.scalar.copy(view[:, h * m_half:(h + 1) * m_half], halves[h][:].rearrange("p j (m t) -> p m j t", t=PACK))
+            return grouped
+
+        def quantize(grouped, width, name):
+            codes = keep.tile([P, width], U32, name=name + "_codes", align_bytes=64)
+            scales = keep.tile([P, width], U8, name=name + "_scales", align_bytes=64)
+            nc.vector.quantize_mx(out=codes[:].bitcast(FP8X4), scales=scales[:], in_=grouped[:])
+            return codes, scales
+
+        def product(acc, still, t, moving):
+            cols = slice(t * P, (t + 1) * P)
+            nc.tensor.matmul_mx(out=acc, lhsT=still[0][:, cols].bitcast(FP8X4), lhsT_scale=still[1][:, cols],
+                                rhs=moving[0][:].bitcast(FP8X4), rhs_scale=moving[1][:], start=True, stop=True)
+
+        offs_s = picked(table_s, U8, offs_t, "offs_s", False)
+        two_s = picked(table_s, U8, two_t, "two_s", False)
+        cand_s = picked(table_s, U8, cand_t, "cand_s", True)
+        w1_q = quantize(round_weight(w1_raw, "w1_grouped"), S, "w1")
+        offs_w = picked(table_w, U32, offs_t, "offs_w", False)
+        two_w = picked(table_w, U32, two_t, "two_w", False)
+        w2_q = quantize(round_weight(w2_raw, "w2_grouped"), S, "w2")
+        cand_w = picked(table_w, U32, cand_t, "cand_w", True)
+
+        def stream(weights, tokens, name):
+            rows = []
+            for t in range(PACK):
+                acc = psum.tile([P, S], F32, name="%s_acc%d" % (name, t), tag="%s%d" % (name, t))
+                product(acc[:], weights, t, tokens)
+                row = keep.tile([P, S], F32, name="%s_row%d" % (name, t))
+                nc.scalar.activation(row[:], acc[:], ACT.Copy, scale=size[:, t:t + 1])
+                rows.append(row)
+            return rows
+
+        y = stream(w1_q, (offs_w, offs_s), "y")
+        d = stream(w2_q, (two_w, two_s), "d")
+
+        s_acc = [psum.tile([P, S], F32, name="s_acc%d" % t, tag="y%d" % t) for t in range(PACK)]
+        s_row = [keep.tile([P, S], F32, name="s_row%d" % t) for t in range(PACK)]
+
+        def fetch(on_vector, target, window, offsets):
+            if on_vector:
+                nc.vector.tensor_copy(target, window[:].indirect(offsets))
+            else:
+                nc.scalar.activation(target, window[:].indirect(offsets), ACT.Copy)
+
+        for c, (c0, width) in enumerate(CHUNKS):
+            cols = slice(c0, c0 + width)
+            entries = slice(c0 // 16, (c0 + width) // 16)
+            y1 = keep.tile([P, PACK, width], F32, name="y1_%d" % c)
+            d2 = keep.tile([P, PACK, width], F32, name="d2_%d" % c)
+            d3 = keep.tile([P, PACK, width], F32, name="d3_%d" % c)
+            for t in range(PACK):
+                fetch(c < 2, y1[:, t, :], y[t], n1_t[:, entries])
+            for t in range(PACK):
+                fetch(False, d2[:, t, :], d[t], n2_t[:, entries])
+            for t in range(PACK):
+                fetch(False, d3[:, t, :], d[t], n3_t[:, entries])
+            for t in range(PACK):
+                nc.vector.scalar_tensor_tensor(y1[:, t, :], y1[:, t, :], -0.5, y[t][:, cols], ALU.mult, ALU.add)
+            nc.vector.tensor_tensor(y1[:], y1[:], d2[:], ALU.min)
+            z = keep.tile([P, width * PACK], BF16, name="z_%d" % c, align_bytes=64)
+            nc.vector.tensor_tensor(
+                z[:].rearrange("p (c i t) -> p c t i", i=4, t=PACK),
+                y1[:].rearrange("p t (c i) -> p c t i", i=4),
+                d3[:].rearrange("p t (c i) -> p c t i", i=4), ALU.max)
+            z_view = z[:].rearrange("p (c t) -> p c t", t=PACK)
+            nc.vector.tensor_tensor(z_view, z_view, sign[:].unsqueeze(1).to_broadcast([P, width, PACK]), ALU.mult)
+            z_q = quantize(z, width, "z%d" % c)
+            for t in range(PACK):
+                product(s_acc[t][:, cols], (cand_w, cand_s), t, z_q)
+                nc.scalar.activation(s_row[t][:, cols], s_acc[t][:, cols], ACT.Copy, scale=0.0625)
+
+        out_rows = out.rearrange("(p t) c -> t p c", t=PACK)
+        for t in range(PACK):
+            minus_pa = keep.tile([P, PAIRS], F32, name="minus_pa%d" % t)
+            pb = keep.tile([P, PAIRS], F32, name="pb%d" % t)
+            rb = keep.tile([P, PAIRS], F32, name="rb%d" % t)
+            nc.scalar.activation(minus_pa[:], s_row[t][:].indirect(n4_t[:]), ACT.Copy, scale=-1.0)
+            fetch(t == 0, pb[:], s_row[t], n5_t[:])
+            result = keep.tile([P, S], F32, name="result%d" % t)
+            nc.vector.scalar_tensor_tensor(rb[:], minus_pa[:], -0.5, pb[:], ALU.mult, ALU.max)
+            nc.vector.tensor_tensor(result[:].indirect(n4_t[:]), pb[:], minus_pa[:], ALU.add)
+            nc.vector.tensor_copy(result[:].indirect(n5_t[:]), rb[:])
+            nc.sync.dma_start(out_rows[t], result[:])

@@ -28,6 +28,7 @@ def tile_picked_twcclampblift_none_p_kernel(tc, x_words, x_scales, w1, w2, gs, o
     with ExitStack() as ctx:
         lists = ctx.enter_context(tc.tile_pool(name="lists", bufs=1))
         keep = ctx.enter_context(tc.tile_pool(name="keep", bufs=1))
+        reused = ctx.enter_context(tc.tile_pool(name="reused", bufs=1))
         psum = ctx.enter_context(tc.psum_pool(name="psum", bufs=1))
 
         def load_list(dram, name):
@@ -39,7 +40,7 @@ def tile_picked_twcclampblift_none_p_kernel(tc, x_words, x_scales, w1, w2, gs, o
             halves = []
             rows = w.rearrange("(p j) c -> p j c", j=PACK)
             for h in range(2):
-                raw = keep.tile([P, PACK, HALF], F32, name="%s_raw%d" % (name, h))
+                raw = keep.tile([P, PACK, HALF], F32, name="%s_raw%d" % (name, h), tag="%s_raw%d" % (name, h))
                 nc.sync.dma_start(raw[:], rows[:, :, h * HALF:(h + 1) * HALF])
                 halves.append(raw)
             return halves
@@ -48,7 +49,7 @@ def tile_picked_twcclampblift_none_p_kernel(tc, x_words, x_scales, w1, w2, gs, o
         two_t = load_list(two, "two")
         cand_t = load_list(cand, "cand")
         gs_t = keep.tile([P, PACK], F32, name="gs_t")
-        nc.sync.dma_start(gs_t[:], gs.rearrange("(p t) o -> p (t o)", t=PACK))
+        nc.gpsimd.dma_start(gs_t[:], gs.rearrange("(p t) o -> p (t o)", t=PACK))
 
         table_s = keep.tile([P, T], U8, name="table_s", align_bytes=64)
         nc.vector.memset(table_s[:].bitcast(I32), 0)
@@ -65,48 +66,47 @@ def tile_picked_twcclampblift_none_p_kernel(tc, x_words, x_scales, w1, w2, gs, o
         n4_t = load_list(n4, "n4")
         n5_t = load_list(n5, "n5")
 
-        twice = keep.tile([P, PACK], F32, name="twice")
-        sign32 = keep.tile([P, PACK], F32, name="sign32")
         sign = keep.tile([P, PACK], BF16, name="sign")
-        size = keep.tile([P, PACK], F32, name="size")
-        nc.gpsimd.tensor_scalar(twice[:], gs_t[:], 0.0, 2.0, ALU.is_ge, ALU.mult)
-        nc.gpsimd.tensor_scalar(sign32[:], twice[:], 1.0, -1.0, ALU.mult, ALU.add)
-        nc.gpsimd.tensor_tensor(size[:], gs_t[:], sign32[:], ALU.mult)
-        nc.gpsimd.tensor_copy(sign[:], sign32[:])
+        nc.scalar.activation(sign[:], gs_t[:], ACT.Sign)
 
-        def picked(table, dtype, offsets, name, dealt):
-            tile = keep.tile([P, S], dtype, name=name, align_bytes=64)
+        def picked(table, dtype, offsets, tile, dealt):
             target = tile[:].rearrange("p (t m) -> p m t", t=PACK) if dealt else tile[:]
             nc.vector.tensor_copy(target, table[:].indirect(offsets[:]))
             return tile
 
-        def round_weight(halves, name):
-            grouped = keep.tile([P, PACK * S], BF16, name=name, align_bytes=64)
-            view = grouped[:].rearrange("p (t m j) -> p m j t", t=PACK, j=PACK)
-            for h in range(2):
-                m_half = HALF // PACK
-                nc.scalar.copy(view[:, h * m_half:(h + 1) * m_half], halves[h][:].rearrange("p j (m t) -> p m j t", t=PACK))
-            return grouped
+        def round_on_scalar(grouped, raw):
+            nc.scalar.copy(grouped.rearrange("p t m j -> p m j t"), raw.rearrange("p t m j -> p m j t"))
 
-        def quantize(grouped, width, name):
+        def round_on_vector(grouped, raw):
+            nc.vector.tensor_copy(grouped.rearrange("p t m j -> p m j t"), raw.rearrange("p t m j -> p m j t"))
+
+        def round_weight(grouped, halves, rounders):
+            view = grouped[:].rearrange("p (t m j) -> p t m j", t=PACK, j=PACK)
+            m_half = HALF // PACK
+            for h, rounder in enumerate(rounders):
+                rounder(view[:, :, h * m_half:(h + 1) * m_half], halves[h][:].rearrange("p j (m t) -> p t m j", t=PACK))
+
+        def mx_tiles(width, name):
             codes = keep.tile([P, width], U32, name=name + "_codes", align_bytes=64)
             scales = keep.tile([P, width], U8, name=name + "_scales", align_bytes=64)
-            nc.vector.quantize_mx(out=codes[:].bitcast(FP8X4), scales=scales[:], in_=grouped[:])
             return codes, scales
+
+        def quantize(target, cols, grouped):
+            nc.vector.quantize_mx(out=target[0][:, cols].bitcast(FP8X4), scales=target[1][:, cols], in_=grouped[:])
 
         def product(acc, still, t, moving):
             cols = slice(t * P, (t + 1) * P)
             nc.tensor.matmul_mx(out=acc, lhsT=still[0][:, cols].bitcast(FP8X4), lhsT_scale=still[1][:, cols],
                                 rhs=moving[0][:].bitcast(FP8X4), rhs_scale=moving[1][:], start=True, stop=True)
 
-        offs_s = picked(table_s, U8, offs_t, "offs_s", False)
-        two_s = picked(table_s, U8, two_t, "two_s", False)
-        cand_s = picked(table_s, U8, cand_t, "cand_s", True)
-        w1_q = quantize(round_weight(w1_raw, "w1_grouped"), S, "w1")
-        offs_w = picked(table_w, U32, offs_t, "offs_w", False)
-        two_w = picked(table_w, U32, two_t, "two_w", False)
-        w2_q = quantize(round_weight(w2_raw, "w2_grouped"), S, "w2")
-        cand_w = picked(table_w, U32, cand_t, "cand_w", True)
+        offs_s = picked(table_s, U8, offs_t, keep.tile([P, S], U8, name="offs_s", align_bytes=64), False)
+        two_s = picked(table_s, U8, two_t, keep.tile([P, S], U8, name="two_s", align_bytes=64), False)
+        cand_s = picked(table_s, U8, cand_t, keep.tile([P, S], U8, name="cand_s", align_bytes=64), True)
+        w1_q = mx_tiles(S, "w1")
+        w1_grouped = keep.tile([P, PACK * S], BF16, name="w1_grouped", tag="after_w1_0", align_bytes=64)
+        round_weight(w1_grouped, w1_raw, (round_on_scalar, round_on_scalar))
+        quantize(w1_q, slice(0, S), w1_grouped)
+        offs_w = picked(table_w, U32, offs_t, keep.tile([P, S], U32, name="offs_w", align_bytes=64), False)
 
         def stream(weights, tokens, name):
             rows = []
@@ -118,10 +118,23 @@ def tile_picked_twcclampblift_none_p_kernel(tc, x_words, x_scales, w1, w2, gs, o
                 rows.append(row)
             return rows
 
+        two_w = picked(table_w, U32, two_t, keep.tile([P, S], U32, name="two_w", tag="after_w1_0", align_bytes=64), False)
+        w2_q = mx_tiles(S, "w2")
+        w2_grouped = reused.tile([P, PACK * S], BF16, name="w2_grouped", align_bytes=64, offset=0)
+        round_weight(w2_grouped, w2_raw, (round_on_scalar, round_on_vector))
+        size = keep.tile([P, PACK], F32, name="size", tag="w2_raw0")
+        nc.scalar.activation(size[:], gs_t[:], ACT.Abs)
         y = stream(w1_q, (offs_w, offs_s), "y")
+        quantize(w2_q, slice(0, S), w2_grouped)
         d = stream(w2_q, (two_w, two_s), "d")
 
-        s_acc = [psum.tile([P, S], F32, name="s_acc%d" % t, tag="y%d" % t) for t in range(PACK)]
+        s_bank = [psum.tile([P, S], F32, name="s_bank%d" % b, tag="y%d" % b) for b in range(PACK)]
+
+        def s_acc(c, t):
+            c0, width = CHUNKS[c]
+            first = c0 * PACK + t * width
+            return s_bank[first // S][:, first % S:first % S + width]
+
         s_row = [keep.tile([P, S], F32, name="s_row%d" % t) for t in range(PACK)]
 
         def fetch(on_vector, target, window, offsets):
@@ -130,42 +143,52 @@ def tile_picked_twcclampblift_none_p_kernel(tc, x_words, x_scales, w1, w2, gs, o
             else:
                 nc.scalar.activation(target, window[:].indirect(offsets), ACT.Copy)
 
+        u = keep.tile([P, PACK, S], F32, name="u")
+        y1 = reused.tile([P, PACK, S], F32, name="y1", align_bytes=64, offset=2048)
+        for t in range(PACK):
+            for h in range(2):
+                fetch(t >= 1, y1[:, t, h * HALF:(h + 1) * HALF], y[t], n1_t[:, h * 16:(h + 1) * 16])
+            nc.vector.scalar_tensor_tensor(u[:, t, :], y1[:, t, :], -0.5, y[t][:], ALU.mult, ALU.add)
+
+        cand_w = picked(table_w, U32, cand_t, reused.tile([P, S], U32, name="cand_w", align_bytes=64, offset=0), True)
+
         for c, (c0, width) in enumerate(CHUNKS):
             cols = slice(c0, c0 + width)
             entries = slice(c0 // 16, (c0 + width) // 16)
-            y1 = keep.tile([P, PACK, width], F32, name="y1_%d" % c)
             d2 = keep.tile([P, PACK, width], F32, name="d2_%d" % c)
             d3 = keep.tile([P, PACK, width], F32, name="d3_%d" % c)
             for t in range(PACK):
-                fetch(c < 2, y1[:, t, :], y[t], n1_t[:, entries])
-            for t in range(PACK):
                 fetch(False, d2[:, t, :], d[t], n2_t[:, entries])
             for t in range(PACK):
-                fetch(False, d3[:, t, :], d[t], n3_t[:, entries])
-            for t in range(PACK):
-                nc.vector.scalar_tensor_tensor(y1[:, t, :], y1[:, t, :], -0.5, y[t][:, cols], ALU.mult, ALU.add)
-            nc.vector.tensor_tensor(y1[:], y1[:], d2[:], ALU.min)
+                fetch(t == 3 and c < 2, d3[:, t, :], d[t], n3_t[:, entries])
+            nc.vector.tensor_tensor(d2[:], d2[:], u[:, :, cols], ALU.min)
             z = keep.tile([P, width * PACK], BF16, name="z_%d" % c, align_bytes=64)
             nc.vector.tensor_tensor(
                 z[:].rearrange("p (c i t) -> p c t i", i=4, t=PACK),
-                y1[:].rearrange("p t (c i) -> p c t i", i=4),
+                d2[:].rearrange("p t (c i) -> p c t i", i=4),
                 d3[:].rearrange("p t (c i) -> p c t i", i=4), ALU.max)
             z_view = z[:].rearrange("p (c t) -> p c t", t=PACK)
             nc.vector.tensor_tensor(z_view, z_view, sign[:].unsqueeze(1).to_broadcast([P, width, PACK]), ALU.mult)
-            z_q = quantize(z, width, "z%d" % c)
+            z_q = mx_tiles(width, "z%d" % c)
+            quantize(z_q, slice(0, width), z)
             for t in range(PACK):
-                product(s_acc[t][:, cols], (cand_w, cand_s), t, z_q)
-                nc.scalar.activation(s_row[t][:, cols], s_acc[t][:, cols], ACT.Copy, scale=0.0625)
+                product(s_acc(c, t), (cand_w, cand_s), t, z_q)
 
         out_rows = out.rearrange("(p t) c -> t p c", t=PACK)
         for t in range(PACK):
+            for c, (c0, width) in enumerate(CHUNKS):
+                nc.scalar.activation(s_row[t][:, c0:c0 + width], s_acc(c, t), ACT.Copy, scale=0.0625)
             minus_pa = keep.tile([P, PAIRS], F32, name="minus_pa%d" % t)
             pb = keep.tile([P, PAIRS], F32, name="pb%d" % t)
             rb = keep.tile([P, PAIRS], F32, name="rb%d" % t)
-            nc.scalar.activation(minus_pa[:], s_row[t][:].indirect(n4_t[:]), ACT.Copy, scale=-1.0)
-            fetch(t == 0, pb[:], s_row[t], n5_t[:])
             result = keep.tile([P, S], F32, name="result%d" % t)
+            pieces = ((0, 128), (128, 128)) if t == 0 else ((0, PAIRS),)
+            for p0, count in pieces:
+                pairs = slice(p0, p0 + count)
+                entries = slice(p0 // 16, (p0 + count) // 16)
+                nc.scalar.activation(minus_pa[:, pairs], s_row[t][:].indirect(n4_t[:, entries]), ACT.Copy, scale=-1.0)
+                fetch(t == 0 and p0 == 0, pb[:, pairs], s_row[t], n5_t[:, entries])
+                nc.vector.tensor_tensor(result[:].indirect(n4_t[:, entries]), pb[:, pairs], minus_pa[:, pairs], ALU.add)
             nc.vector.scalar_tensor_tensor(rb[:], minus_pa[:], -0.5, pb[:], ALU.mult, ALU.max)
-            nc.vector.tensor_tensor(result[:].indirect(n4_t[:]), pb[:], minus_pa[:], ALU.add)
             nc.vector.tensor_copy(result[:].indirect(n5_t[:]), rb[:])
             nc.sync.dma_start(out_rows[t], result[:])

@@ -48,8 +48,6 @@ def tile_picked_twcclampblift_none_p_kernel(tc, x_words, x_scales, w1, w2, gs, o
         offs_t = load_list(offs, "offs")
         two_t = load_list(two, "two")
         cand_t = load_list(cand, "cand")
-        gs_t = keep.tile([P, PACK], F32, name="gs_t")
-        nc.gpsimd.dma_start(gs_t[:], gs.rearrange("(p t) o -> p (t o)", t=PACK))
 
         table_s = keep.tile([P, T], U8, name="table_s", align_bytes=64)
         nc.vector.memset(table_s[:].bitcast(I32), 0)
@@ -59,6 +57,8 @@ def tile_picked_twcclampblift_none_p_kernel(tc, x_words, x_scales, w1, w2, gs, o
         w1_raw = load_weight(w1, "w1")
         table_w = keep.tile([P, T], U32, name="table_w", align_bytes=64)
         nc.sync.dma_start(table_w[:].bitcast(I32), x_words[0].rearrange("p n t -> p (n t)").bitcast(I32))
+        gs_t = keep.tile([P, PACK], F32, name="gs_t")
+        nc.sync.dma_start(gs_t[:], gs.rearrange("(p t) o -> p (t o)", t=PACK))
         w2_raw = load_weight(w2, "w2")
         n1_t = load_list(n1, "n1")
         n2_t = load_list(n2, "n2")
@@ -69,16 +69,21 @@ def tile_picked_twcclampblift_none_p_kernel(tc, x_words, x_scales, w1, w2, gs, o
         sign = keep.tile([P, PACK], BF16, name="sign")
         nc.scalar.activation(sign[:], gs_t[:], ACT.Sign)
 
-        def picked(table, dtype, offsets, tile, dealt):
-            target = tile[:].rearrange("p (t m) -> p m t", t=PACK) if dealt else tile[:]
-            nc.vector.tensor_copy(target, table[:].indirect(offsets[:]))
+        def picked(table, offsets, tile):
+            nc.vector.tensor_copy(tile[:], table[:].indirect(offsets[:]))
+            return tile
+
+        def dealt(source, dtype, run, name):
+            tile = keep.tile([P, S], dtype, name=name, align_bytes=64)
+            nc.vector.tensor_copy(tile[:].rearrange("p (t b i) -> p b t i", t=PACK, i=run),
+                                  source[:].rearrange("p (b i t) -> p b t i", t=PACK, i=run))
             return tile
 
         def round_on_scalar(grouped, raw):
             nc.scalar.copy(grouped.rearrange("p t m j -> p m j t"), raw.rearrange("p t m j -> p m j t"))
 
         def round_on_vector(grouped, raw):
-            nc.vector.tensor_copy(grouped.rearrange("p t m j -> p m j t"), raw.rearrange("p t m j -> p m j t"))
+            nc.vector.tensor_copy(grouped.rearrange("p t m j -> p m t j"), raw.rearrange("p t m j -> p m t j"))
 
         def round_weight(grouped, halves, rounders):
             view = grouped[:].rearrange("p (t m j) -> p t m j", t=PACK, j=PACK)
@@ -99,14 +104,14 @@ def tile_picked_twcclampblift_none_p_kernel(tc, x_words, x_scales, w1, w2, gs, o
             nc.tensor.matmul_mx(out=acc, lhsT=still[0][:, cols].bitcast(FP8X4), lhsT_scale=still[1][:, cols],
                                 rhs=moving[0][:].bitcast(FP8X4), rhs_scale=moving[1][:], start=True, stop=True)
 
-        offs_s = picked(table_s, U8, offs_t, keep.tile([P, S], U8, name="offs_s", align_bytes=64), False)
-        two_s = picked(table_s, U8, two_t, keep.tile([P, S], U8, name="two_s", align_bytes=64), False)
-        cand_s = picked(table_s, U8, cand_t, keep.tile([P, S], U8, name="cand_s", align_bytes=64), True)
+        offs_s = picked(table_s, offs_t, keep.tile([P, S], U8, name="offs_s", align_bytes=64))
+        two_s = picked(table_s, two_t, keep.tile([P, S], U8, name="two_s", align_bytes=64))
+        cand_s = dealt(picked(table_s, cand_t, keep.tile([P, S], U8, name="cand_s", align_bytes=64)), U8, 16, "cand_s_dealt")
         w1_q = mx_tiles(S, "w1")
         w1_grouped = keep.tile([P, PACK * S], BF16, name="w1_grouped", tag="after_w1_0", align_bytes=64)
         round_weight(w1_grouped, w1_raw, (round_on_scalar, round_on_scalar))
         quantize(w1_q, slice(0, S), w1_grouped)
-        offs_w = picked(table_w, U32, offs_t, keep.tile([P, S], U32, name="offs_w", align_bytes=64), False)
+        offs_w = picked(table_w, offs_t, keep.tile([P, S], U32, name="offs_w", align_bytes=64))
 
         def stream(weights, tokens, name):
             rows = []
@@ -118,7 +123,7 @@ def tile_picked_twcclampblift_none_p_kernel(tc, x_words, x_scales, w1, w2, gs, o
                 rows.append(row)
             return rows
 
-        two_w = picked(table_w, U32, two_t, keep.tile([P, S], U32, name="two_w", tag="after_w1_0", align_bytes=64), False)
+        two_w = picked(table_w, two_t, keep.tile([P, S], U32, name="two_w", tag="after_w1_0", align_bytes=64))
         w2_q = mx_tiles(S, "w2")
         w2_grouped = reused.tile([P, PACK * S], BF16, name="w2_grouped", align_bytes=64, offset=0)
         round_weight(w2_grouped, w2_raw, (round_on_scalar, round_on_vector))
@@ -150,7 +155,7 @@ def tile_picked_twcclampblift_none_p_kernel(tc, x_words, x_scales, w1, w2, gs, o
                 fetch(t >= 1, y1[:, t, h * HALF:(h + 1) * HALF], y[t], n1_t[:, h * 16:(h + 1) * 16])
             nc.vector.scalar_tensor_tensor(u[:, t, :], y1[:, t, :], -0.5, y[t][:], ALU.mult, ALU.add)
 
-        cand_w = picked(table_w, U32, cand_t, reused.tile([P, S], U32, name="cand_w", align_bytes=64, offset=0), True)
+        cand_w = dealt(picked(table_w, cand_t, reused.tile([P, S], U32, name="cand_w", align_bytes=64, offset=0)), U32, 4, "cand_w_dealt")
 
         for c, (c0, width) in enumerate(CHUNKS):
             cols = slice(c0, c0 + width)
@@ -160,13 +165,13 @@ def tile_picked_twcclampblift_none_p_kernel(tc, x_words, x_scales, w1, w2, gs, o
             for t in range(PACK):
                 fetch(False, d2[:, t, :], d[t], n2_t[:, entries])
             for t in range(PACK):
-                fetch(t == 3 and c < 2, d3[:, t, :], d[t], n3_t[:, entries])
+                fetch(t == 3 and c == 0, d3[:, t, :], d[t], n3_t[:, entries])
             nc.vector.tensor_tensor(d2[:], d2[:], u[:, :, cols], ALU.min)
             z = keep.tile([P, width * PACK], BF16, name="z_%d" % c, align_bytes=64)
             nc.vector.tensor_tensor(
-                z[:].rearrange("p (c i t) -> p c t i", i=4, t=PACK),
-                d2[:].rearrange("p t (c i) -> p c t i", i=4),
-                d3[:].rearrange("p t (c i) -> p c t i", i=4), ALU.max)
+                z[:].rearrange("p (c i t) -> p c t i", i=2, t=PACK),
+                d2[:].rearrange("p t (c i) -> p c t i", i=2),
+                d3[:].rearrange("p t (c i) -> p c t i", i=2), ALU.max)
             z_view = z[:].rearrange("p (c t) -> p c t", t=PACK)
             nc.vector.tensor_tensor(z_view, z_view, sign[:].unsqueeze(1).to_broadcast([P, width, PACK]), ALU.mult)
             z_q = mx_tiles(width, "z%d" % c)

@@ -1,6 +1,7 @@
 from contextlib import ExitStack
 
 import concourse.mybir as mybir
+from concourse.masks import make_identity
 
 F32 = mybir.dt.float32
 BF16 = mybir.dt.bfloat16
@@ -17,8 +18,13 @@ PACK = 4
 T = 2048
 S = 512
 PAIRS = 256
-HALF = 256
-CHUNKS = ((0, 256), (256, 128), (384, 128))
+HALF = S // 2
+STRIPE = 16
+LINE_BYTES = 16
+QUADRANT = 32
+STRETCHES = ((0, 256), (256, 128), (384, 128))
+N1_ON_VECTOR_FROM = 1
+FIRST_TILE_PIECES = ((0, 128), (128, 128))
 
 FLOPS = 3 * 2 * 512 * 512 * 512
 
@@ -45,14 +51,18 @@ def tile_picked_twcclampblift_none_p_kernel(tc, x_words, x_scales, w1, w2, gs, o
                 halves.append(raw)
             return halves
 
+        def entries(offsets, first, count):
+            return offsets[:, first // STRIPE:(first + count) // STRIPE]
+
         offs_t = load_list(offs, "offs")
         two_t = load_list(two, "two")
         cand_t = load_list(cand, "cand")
 
         table_s = keep.tile([P, T], U8, name="table_s", align_bytes=64)
         nc.vector.memset(table_s[:].bitcast(I32), 0)
-        for q in range(4):
-            nc.sync.dma_start(table_s[32 * q:32 * q + 4, :].bitcast(I32), x_scales[0, 4 * q:4 * q + 4, :].bitcast(I32))
+        for q in range(P // QUADRANT):
+            nc.sync.dma_start(table_s[QUADRANT * q:QUADRANT * q + 4, :].bitcast(I32),
+                              x_scales[0, 4 * q:4 * q + 4, :].bitcast(I32))
 
         w1_raw = load_weight(w1, "w1")
         table_w = keep.tile([P, T], U32, name="table_w", align_bytes=64)
@@ -66,14 +76,18 @@ def tile_picked_twcclampblift_none_p_kernel(tc, x_words, x_scales, w1, w2, gs, o
         n4_t = load_list(n4, "n4")
         n5_t = load_list(n5, "n5")
 
-        sign = keep.tile([P, PACK], BF16, name="sign")
-        nc.scalar.activation(sign[:], gs_t[:], ACT.Sign)
+        identity = keep.tile([P, P], F32, name="identity")
+        make_identity(nc, identity[:])
+
+        gs_sign = keep.tile([P, PACK], BF16, name="gs_sign")
+        nc.scalar.activation(gs_sign[:], gs_t[:], ACT.Sign)
 
         def picked(table, offsets, tile):
             nc.vector.tensor_copy(tile[:], table[:].indirect(offsets[:]))
             return tile
 
-        def dealt(source, dtype, run, name):
+        def dealt(source, dtype, item_bytes, name):
+            run = LINE_BYTES // item_bytes
             tile = keep.tile([P, S], dtype, name=name, align_bytes=64)
             nc.vector.tensor_copy(tile[:].rearrange("p (t b i) -> p b t i", t=PACK, i=run),
                                   source[:].rearrange("p (b i t) -> p b t i", t=PACK, i=run))
@@ -91,56 +105,16 @@ def tile_picked_twcclampblift_none_p_kernel(tc, x_words, x_scales, w1, w2, gs, o
             for h, rounder in enumerate(rounders):
                 rounder(view[:, :, h * m_half:(h + 1) * m_half], halves[h][:].rearrange("p j (m t) -> p t m j", t=PACK))
 
-        def mx_tiles(width, name):
+        def quantized(grouped, width, name):
             codes = keep.tile([P, width], U32, name=name + "_codes", align_bytes=64)
             scales = keep.tile([P, width], U8, name=name + "_scales", align_bytes=64)
+            nc.vector.quantize_mx(out=codes[:].bitcast(FP8X4), scales=scales[:], in_=grouped[:])
             return codes, scales
 
-        def quantize(target, cols, grouped):
-            nc.vector.quantize_mx(out=target[0][:, cols].bitcast(FP8X4), scales=target[1][:, cols], in_=grouped[:])
-
-        def product(acc, still, t, moving):
+        def product(acc, stationary, t, moving):
             cols = slice(t * P, (t + 1) * P)
-            nc.tensor.matmul_mx(out=acc, lhsT=still[0][:, cols].bitcast(FP8X4), lhsT_scale=still[1][:, cols],
+            nc.tensor.matmul_mx(out=acc, lhsT=stationary[0][:, cols].bitcast(FP8X4), lhsT_scale=stationary[1][:, cols],
                                 rhs=moving[0][:].bitcast(FP8X4), rhs_scale=moving[1][:], start=True, stop=True)
-
-        offs_s = picked(table_s, offs_t, keep.tile([P, S], U8, name="offs_s", align_bytes=64))
-        two_s = picked(table_s, two_t, keep.tile([P, S], U8, name="two_s", align_bytes=64))
-        cand_s = dealt(picked(table_s, cand_t, keep.tile([P, S], U8, name="cand_s", align_bytes=64)), U8, 16, "cand_s_dealt")
-        w1_q = mx_tiles(S, "w1")
-        w1_grouped = keep.tile([P, PACK * S], BF16, name="w1_grouped", tag="after_w1_0", align_bytes=64)
-        round_weight(w1_grouped, w1_raw, (round_on_scalar, round_on_scalar))
-        quantize(w1_q, slice(0, S), w1_grouped)
-        offs_w = picked(table_w, offs_t, keep.tile([P, S], U32, name="offs_w", align_bytes=64))
-
-        def stream(weights, tokens, name):
-            rows = []
-            for t in range(PACK):
-                acc = psum.tile([P, S], F32, name="%s_acc%d" % (name, t), tag="%s%d" % (name, t))
-                product(acc[:], weights, t, tokens)
-                row = keep.tile([P, S], F32, name="%s_row%d" % (name, t))
-                nc.scalar.activation(row[:], acc[:], ACT.Copy, scale=size[:, t:t + 1])
-                rows.append(row)
-            return rows
-
-        two_w = picked(table_w, two_t, keep.tile([P, S], U32, name="two_w", tag="after_w1_0", align_bytes=64))
-        w2_q = mx_tiles(S, "w2")
-        w2_grouped = reused.tile([P, PACK * S], BF16, name="w2_grouped", align_bytes=64, offset=0)
-        round_weight(w2_grouped, w2_raw, (round_on_scalar, round_on_vector))
-        size = keep.tile([P, PACK], F32, name="size", tag="w2_raw0")
-        nc.scalar.activation(size[:], gs_t[:], ACT.Abs)
-        y = stream(w1_q, (offs_w, offs_s), "y")
-        quantize(w2_q, slice(0, S), w2_grouped)
-        d = stream(w2_q, (two_w, two_s), "d")
-
-        s_bank = [psum.tile([P, S], F32, name="s_bank%d" % b, tag="y%d" % b) for b in range(PACK)]
-
-        def s_acc(c, t):
-            c0, width = CHUNKS[c]
-            first = c0 * PACK + t * width
-            return s_bank[first // S][:, first % S:first % S + width]
-
-        s_row = [keep.tile([P, S], F32, name="s_row%d" % t) for t in range(PACK)]
 
         def fetch(on_vector, target, window, offsets):
             if on_vector:
@@ -148,52 +122,103 @@ def tile_picked_twcclampblift_none_p_kernel(tc, x_words, x_scales, w1, w2, gs, o
             else:
                 nc.scalar.activation(target, window[:].indirect(offsets), ACT.Copy)
 
+        offs_s = picked(table_s, offs_t, keep.tile([P, S], U8, name="offs_s", align_bytes=64))
+        two_s = picked(table_s, two_t, keep.tile([P, S], U8, name="two_s", align_bytes=64))
+        cand_s = dealt(picked(table_s, cand_t, keep.tile([P, S], U8, name="cand_s", align_bytes=64)), U8, 1, "cand_s_dealt")
+        w1_grouped = keep.tile([P, PACK * S], BF16, name="w1_grouped", tag="w1_grouped", align_bytes=64)
+        round_weight(w1_grouped, w1_raw, (round_on_scalar, round_on_scalar))
+        w1_q = quantized(w1_grouped, S, "w1")
+        offs_w = picked(table_w, offs_t, keep.tile([P, S], U32, name="offs_w", align_bytes=64))
+
+        two_w = picked(table_w, two_t, keep.tile([P, S], U32, name="two_w", tag="w1_grouped", align_bytes=64))
+        w2_grouped = reused.tile([P, PACK * S], BF16, name="w2_grouped", align_bytes=64, offset=0)
+        round_weight(w2_grouped, w2_raw, (round_on_scalar, round_on_vector))
+        gs_size = keep.tile([P, PACK], F32, name="gs_size", tag="w2_raw0")
+        nc.scalar.activation(gs_size[:], gs_t[:], ACT.Abs)
+
+        def stream(weights, tokens, name):
+            rows = []
+            for t in range(PACK):
+                acc = psum.tile([P, S], F32, name="%s_acc%d" % (name, t), tag="%s%d" % (name, t))
+                product(acc[:], weights, t, tokens)
+                row = keep.tile([P, S], F32, name="%s_row%d" % (name, t))
+                nc.scalar.activation(row[:], acc[:], ACT.Copy, scale=gs_size[:, t:t + 1])
+                rows.append(row)
+            return rows
+
+        y = stream(w1_q, (offs_w, offs_s), "y")
+        w2_q = quantized(w2_grouped, S, "w2")
+        d = stream(w2_q, (two_w, two_s), "d")
+
+        s_bank = [psum.tile([P, S], F32, name="s_bank%d" % b, tag="y%d" % b) for b in range(PACK)]
+
+        def s_acc(c, t):
+            first, width = STRETCHES[c]
+            start = first * PACK + t * width
+            return s_bank[start // S][:, start % S:start % S + width]
+
+        s_row = [keep.tile([P, S], F32, name="s_row%d" % t) for t in range(PACK)]
+
         u = keep.tile([P, PACK, S], F32, name="u")
-        y1 = reused.tile([P, PACK, S], F32, name="y1", align_bytes=64, offset=2048)
+        y_at_n1 = reused.tile([P, PACK, S], F32, name="y_at_n1", align_bytes=64, offset=S * 4)
         for t in range(PACK):
             for h in range(2):
-                fetch(t >= 1, y1[:, t, h * HALF:(h + 1) * HALF], y[t], n1_t[:, h * 16:(h + 1) * 16])
-            nc.vector.scalar_tensor_tensor(u[:, t, :], y1[:, t, :], -0.5, y[t][:], ALU.mult, ALU.add)
+                fetch(t >= N1_ON_VECTOR_FROM, y_at_n1[:, t, h * HALF:(h + 1) * HALF], y[t], entries(n1_t, h * HALF, HALF))
+            nc.vector.scalar_tensor_tensor(u[:, t, :], y_at_n1[:, t, :], -0.5, y[t][:], ALU.mult, ALU.add)
 
-        cand_w = dealt(picked(table_w, cand_t, reused.tile([P, S], U32, name="cand_w", align_bytes=64, offset=0)), U32, 4, "cand_w_dealt")
+        cand_w = dealt(picked(table_w, cand_t, reused.tile([P, S], U32, name="cand_w", align_bytes=64, offset=0)),
+                       U32, 4, "cand_w_dealt")
 
-        for c, (c0, width) in enumerate(CHUNKS):
-            cols = slice(c0, c0 + width)
-            entries = slice(c0 // 16, (c0 + width) // 16)
-            d2 = keep.tile([P, PACK, width], F32, name="d2_%d" % c)
-            d3 = keep.tile([P, PACK, width], F32, name="d3_%d" % c)
+        for c, (first, width) in enumerate(STRETCHES):
+            low = keep.tile([P, PACK, width], F32, name="low%d" % c)
+            d_at_n3 = keep.tile([P, PACK, width], F32, name="d_at_n3_%d" % c)
             for t in range(PACK):
-                fetch(False, d2[:, t, :], d[t], n2_t[:, entries])
+                fetch(False, low[:, t, :], d[t], entries(n2_t, first, width))
             for t in range(PACK):
-                fetch(t == 3 and c == 0, d3[:, t, :], d[t], n3_t[:, entries])
-            nc.vector.tensor_tensor(d2[:], d2[:], u[:, :, cols], ALU.min)
-            z = keep.tile([P, width * PACK], BF16, name="z_%d" % c, align_bytes=64)
+                fetch(t == PACK - 1 and c == 0, d_at_n3[:, t, :], d[t], entries(n3_t, first, width))
+            nc.vector.tensor_tensor(low[:], low[:], u[:, :, first:first + width], ALU.min)
+            z = keep.tile([P, width * PACK], BF16, name="z%d" % c, align_bytes=64)
             nc.vector.tensor_tensor(
                 z[:].rearrange("p (c i t) -> p c t i", i=2, t=PACK),
-                d2[:].rearrange("p t (c i) -> p c t i", i=2),
-                d3[:].rearrange("p t (c i) -> p c t i", i=2), ALU.max)
+                low[:].rearrange("p t (c i) -> p c t i", i=2),
+                d_at_n3[:].rearrange("p t (c i) -> p c t i", i=2), ALU.max)
             z_view = z[:].rearrange("p (c t) -> p c t", t=PACK)
-            nc.vector.tensor_tensor(z_view, z_view, sign[:].unsqueeze(1).to_broadcast([P, width, PACK]), ALU.mult)
-            z_q = mx_tiles(width, "z%d" % c)
-            quantize(z_q, slice(0, width), z)
+            nc.vector.tensor_tensor(z_view, z_view, gs_sign[:].unsqueeze(1).to_broadcast([P, width, PACK]), ALU.mult)
+            z_q = quantized(z, width, "z%d" % c)
             for t in range(PACK):
                 product(s_acc(c, t), (cand_w, cand_s), t, z_q)
 
         out_rows = out.rearrange("(p t) c -> t p c", t=PACK)
         for t in range(PACK):
-            for c, (c0, width) in enumerate(CHUNKS):
-                nc.scalar.activation(s_row[t][:, c0:c0 + width], s_acc(c, t), ACT.Copy, scale=0.0625)
+            for c, (first, width) in enumerate(STRETCHES):
+                nc.scalar.activation(s_row[t][:, first:first + width], s_acc(c, t), ACT.Copy, scale=0.0625)
             minus_pa = keep.tile([P, PAIRS], F32, name="minus_pa%d" % t)
             pb = keep.tile([P, PAIRS], F32, name="pb%d" % t)
-            rb = keep.tile([P, PAIRS], F32, name="rb%d" % t)
             result = keep.tile([P, S], F32, name="result%d" % t)
-            pieces = ((0, 128), (128, 128)) if t == 0 else ((0, PAIRS),)
-            for p0, count in pieces:
-                pairs = slice(p0, p0 + count)
-                entries = slice(p0 // 16, (p0 + count) // 16)
-                nc.scalar.activation(minus_pa[:, pairs], s_row[t][:].indirect(n4_t[:, entries]), ACT.Copy, scale=-1.0)
-                fetch(t == 0 and p0 == 0, pb[:, pairs], s_row[t], n5_t[:, entries])
-                nc.vector.tensor_tensor(result[:].indirect(n4_t[:, entries]), pb[:, pairs], minus_pa[:, pairs], ALU.add)
-            nc.vector.scalar_tensor_tensor(rb[:], minus_pa[:], -0.5, pb[:], ALU.mult, ALU.max)
-            nc.vector.tensor_copy(result[:].indirect(n5_t[:]), rb[:])
+            for first, count in FIRST_TILE_PIECES if t == 0 else ((0, PAIRS),):
+                pairs = slice(first, first + count)
+                nc.scalar.activation(minus_pa[:, pairs], s_row[t][:].indirect(entries(n4_t, first, count)), ACT.Copy, scale=-1.0)
+                fetch(t == 0 and first == 0, pb[:, pairs], s_row[t], entries(n5_t, first, count))
+                nc.vector.tensor_tensor(result[:].indirect(entries(n4_t, first, count)), pb[:, pairs], minus_pa[:, pairs], ALU.add)
+            if t == 0:
+                rb = keep.tile([P, PAIRS], F32, name="rb")
+                nc.vector.scalar_tensor_tensor(rb[:], minus_pa[:], -0.5, pb[:], ALU.mult, ALU.max)
+                nc.vector.tensor_copy(result[:].indirect(n5_t[:]), rb[:])
+            else:
+                turned = psum.tile([P, PAIRS], F32, name="turned%d" % t, tag="d%d" % (2 * t % PACK))
+                back = psum.tile([P, PAIRS], F32, name="back%d" % t, tag="d%d" % ((2 * t + 1) % PACK))
+                lift_turned = keep.tile([P, PAIRS], F32, name="lift_turned%d" % t)
+                lift = keep.tile([P, PAIRS], F32, name="lift%d" % t)
+                terms = (pb, pb, minus_pa)
+                for b in range(PAIRS // P):
+                    block = slice(b * P, (b + 1) * P)
+                    for n, term in enumerate(terms):
+                        nc.tensor.matmul(turned[:, block], term[:, block], identity[:],
+                                         start=n == 0, stop=n == len(terms) - 1, is_transpose=True)
+                nc.scalar.activation(lift_turned[:], turned[:], ACT.Relu, scale=-0.5)
+                for b in range(PAIRS // P):
+                    block = slice(b * P, (b + 1) * P)
+                    nc.tensor.transpose(back[:, block], lift_turned[:, block], identity[:])
+                nc.scalar.copy(lift[:], back[:])
+                nc.vector.tensor_tensor(result[:].indirect(n5_t[:]), pb[:], lift[:], ALU.add)
             nc.sync.dma_start(out_rows[t], result[:])

from contextlib import ExitStack

import concourse.mybir as mybir
from concourse.masks import make_identity

F32 = mybir.dt.float32
BF16 = mybir.dt.bfloat16
I32 = mybir.dt.int32
U32 = mybir.dt.uint32
U16 = mybir.dt.uint16
U8 = mybir.dt.uint8
FP8X4 = mybir.dt.float8_e4m3fn_x4
ALU = mybir.AluOpType
ACT = mybir.ActivationFunctionType

P = 128
PACK = 4
T = 2048
S = 512
PAIRS = 256
HALF = S // 2
STRIPE = 16
LINE_BYTES = 16
QUADRANT = 32
STRETCHES = ((0, 256), (256, 128), (384, 128))
N1_ON_VECTOR_FROM = 1
FIRST_TILE_PIECES = ((0, 128), (128, 128))

FLOPS = 3 * 2 * 512 * 512 * 512


def tile_picked_twcclampblift_none_p_kernel(tc, x_words, x_scales, w1, w2, gs, offs, two, n1, n2, n3, cand, n4, n5, out):
    nc = tc.nc
    with ExitStack() as ctx:
        lists = ctx.enter_context(tc.tile_pool(name="lists", bufs=1))
        keep = ctx.enter_context(tc.tile_pool(name="keep", bufs=1))
        reused = ctx.enter_context(tc.tile_pool(name="reused", bufs=1))
        psum = ctx.enter_context(tc.psum_pool(name="psum", bufs=1))

        def load_list(dram, name):
            tile = lists.tile(list(dram.shape), U16, name=name)
            nc.sync.dma_start(tile[:], dram)
            return tile

        def load_weight(w, name):
            halves = []
            rows = w.rearrange("(p j) c -> p j c", j=PACK)
            for h in range(2):
                raw = keep.tile([P, PACK, HALF], F32, name="%s_raw%d" % (name, h), tag="%s_raw%d" % (name, h))
                nc.sync.dma_start(raw[:], rows[:, :, h * HALF:(h + 1) * HALF])
                halves.append(raw)
            return halves

        def entries(offsets, first, count):
            return offsets[:, first // STRIPE:(first + count) // STRIPE]

        offs_t = load_list(offs, "offs")
        two_t = load_list(two, "two")
        cand_t = load_list(cand, "cand")

        table_s = keep.tile([P, T], U8, name="table_s", align_bytes=64)
        nc.vector.memset(table_s[:].bitcast(I32), 0)
        for q in range(P // QUADRANT):
            nc.sync.dma_start(table_s[QUADRANT * q:QUADRANT * q + 4, :].bitcast(I32),
                              x_scales[0, 4 * q:4 * q + 4, :].bitcast(I32))

        w1_raw = load_weight(w1, "w1")
        table_w = keep.tile([P, T], U32, name="table_w", align_bytes=64)
        nc.sync.dma_start(table_w[:].bitcast(I32), x_words[0].rearrange("p n t -> p (n t)").bitcast(I32))
        gs_t = keep.tile([P, PACK], F32, name="gs_t")
        nc.sync.dma_start(gs_t[:], gs.rearrange("(p t) o -> p (t o)", t=PACK))
        w2_raw = load_weight(w2, "w2")
        n1_t = load_list(n1, "n1")
        n2_t = load_list(n2, "n2")
        n3_t = load_list(n3, "n3")
        n4_t = load_list(n4, "n4")
        n5_t = load_list(n5, "n5")

        identity = keep.tile([P, P], F32, name="identity")
        make_identity(nc, identity[:])

        gs_sign = keep.tile([P, PACK], BF16, name="gs_sign")
        nc.scalar.activation(gs_sign[:], gs_t[:], ACT.Sign)

        def picked(table, offsets, tile):
            nc.vector.tensor_copy(tile[:], table[:].indirect(offsets[:]))
            return tile

        def dealt(source, dtype, item_bytes, name):
            run = LINE_BYTES // item_bytes
            tile = keep.tile([P, S], dtype, name=name, align_bytes=64)
            nc.vector.tensor_copy(tile[:].rearrange("p (t b i) -> p b t i", t=PACK, i=run),
                                  source[:].rearrange("p (b i t) -> p b t i", t=PACK, i=run))
            return tile

        def round_on_scalar(grouped, raw):
            nc.scalar.copy(grouped.rearrange("p t m j -> p m j t"), raw.rearrange("p t m j -> p m j t"))

        def round_on_vector(grouped, raw):
            nc.vector.tensor_copy(grouped.rearrange("p t m j -> p m t j"), raw.rearrange("p t m j -> p m t j"))

        def round_weight(grouped, halves, rounders):
            view = grouped[:].rearrange("p (t m j) -> p t m j", t=PACK, j=PACK)
            m_half = HALF // PACK
            for h, rounder in enumerate(rounders):
                rounder(view[:, :, h * m_half:(h + 1) * m_half], halves[h][:].rearrange("p j (m t) -> p t m j", t=PACK))

        def quantized(grouped, width, name):
            codes = keep.tile([P, width], U32, name=name + "_codes", align_bytes=64)
            scales = keep.tile([P, width], U8, name=name + "_scales", align_bytes=64)
            nc.vector.quantize_mx(out=codes[:].bitcast(FP8X4), scales=scales[:], in_=grouped[:])
            return codes, scales

        def product(acc, stationary, t, moving):
            cols = slice(t * P, (t + 1) * P)
            nc.tensor.matmul_mx(out=acc, lhsT=stationary[0][:, cols].bitcast(FP8X4), lhsT_scale=stationary[1][:, cols],
                                rhs=moving[0][:].bitcast(FP8X4), rhs_scale=moving[1][:], start=True, stop=True)

        def fetch(on_vector, target, window, offsets):
            if on_vector:
                nc.vector.tensor_copy(target, window[:].indirect(offsets))
            else:
                nc.scalar.activation(target, window[:].indirect(offsets), ACT.Copy)

        offs_s = picked(table_s, offs_t, keep.tile([P, S], U8, name="offs_s", align_bytes=64))
        two_s = picked(table_s, two_t, keep.tile([P, S], U8, name="two_s", align_bytes=64))
        cand_s = dealt(picked(table_s, cand_t, keep.tile([P, S], U8, name="cand_s", align_bytes=64)), U8, 1, "cand_s_dealt")
        w1_grouped = keep.tile([P, PACK * S], BF16, name="w1_grouped", tag="w1_grouped", align_bytes=64)
        round_weight(w1_grouped, w1_raw, (round_on_scalar, round_on_scalar))
        w1_q = quantized(w1_grouped, S, "w1")
        offs_w = picked(table_w, offs_t, keep.tile([P, S], U32, name="offs_w", align_bytes=64))

        two_w = picked(table_w, two_t, keep.tile([P, S], U32, name="two_w", tag="w1_grouped", align_bytes=64))
        w2_grouped = reused.tile([P, PACK * S], BF16, name="w2_grouped", align_bytes=64, offset=0)
        round_weight(w2_grouped, w2_raw, (round_on_scalar, round_on_vector))
        gs_size = keep.tile([P, PACK], F32, name="gs_size", tag="w2_raw0")
        nc.scalar.activation(gs_size[:], gs_t[:], ACT.Abs)

        def stream(weights, tokens, name):
            rows = []
            for t in range(PACK):
                acc = psum.tile([P, S], F32, name="%s_acc%d" % (name, t), tag="%s%d" % (name, t))
                product(acc[:], weights, t, tokens)
                row = keep.tile([P, S], F32, name="%s_row%d" % (name, t))
                nc.scalar.activation(row[:], acc[:], ACT.Copy, scale=gs_size[:, t:t + 1])
                rows.append(row)
            return rows

        y = stream(w1_q, (offs_w, offs_s), "y")
        w2_q = quantized(w2_grouped, S, "w2")
        d = stream(w2_q, (two_w, two_s), "d")

        s_bank = [psum.tile([P, S], F32, name="s_bank%d" % b, tag="y%d" % b) for b in range(PACK)]

        def s_acc(c, t):
            first, width = STRETCHES[c]
            start = first * PACK + t * width
            return s_bank[start // S][:, start % S:start % S + width]

        s_row = [keep.tile([P, S], F32, name="s_row%d" % t) for t in range(PACK)]

        u = keep.tile([P, PACK, S], F32, name="u")
        y_at_n1 = reused.tile([P, PACK, S], F32, name="y_at_n1", align_bytes=64, offset=S * 4)
        for t in range(PACK):
            for h in range(2):
                fetch(t >= N1_ON_VECTOR_FROM, y_at_n1[:, t, h * HALF:(h + 1) * HALF], y[t], entries(n1_t, h * HALF, HALF))
            nc.vector.scalar_tensor_tensor(u[:, t, :], y_at_n1[:, t, :], -0.5, y[t][:], ALU.mult, ALU.add)

        cand_w = dealt(picked(table_w, cand_t, reused.tile([P, S], U32, name="cand_w", align_bytes=64, offset=0)),
                       U32, 4, "cand_w_dealt")

        for c, (first, width) in enumerate(STRETCHES):
            low = keep.tile([P, PACK, width], F32, name="low%d" % c)
            d_at_n3 = keep.tile([P, PACK, width], F32, name="d_at_n3_%d" % c)
            for t in range(PACK):
                fetch(False, low[:, t, :], d[t], entries(n2_t, first, width))
            for t in range(PACK):
                fetch(t == PACK - 1 and c == 0, d_at_n3[:, t, :], d[t], entries(n3_t, first, width))
            nc.vector.tensor_tensor(low[:], low[:], u[:, :, first:first + width], ALU.min)
            z = keep.tile([P, width * PACK], BF16, name="z%d" % c, align_bytes=64)
            nc.vector.tensor_tensor(
                z[:].rearrange("p (c i t) -> p c t i", i=2, t=PACK),
                low[:].rearrange("p t (c i) -> p c t i", i=2),
                d_at_n3[:].rearrange("p t (c i) -> p c t i", i=2), ALU.max)
            z_view = z[:].rearrange("p (c t) -> p c t", t=PACK)
            nc.vector.tensor_tensor(z_view, z_view, gs_sign[:].unsqueeze(1).to_broadcast([P, width, PACK]), ALU.mult)
            z_q = quantized(z, width, "z%d" % c)
            for t in range(PACK):
                product(s_acc(c, t), (cand_w, cand_s), t, z_q)

        out_rows = out.rearrange("(p t) c -> t p c", t=PACK)
        for t in range(PACK):
            for c, (first, width) in enumerate(STRETCHES):
                nc.scalar.activation(s_row[t][:, first:first + width], s_acc(c, t), ACT.Copy, scale=0.0625)
            minus_pa = keep.tile([P, PAIRS], F32, name="minus_pa%d" % t)
            pb = keep.tile([P, PAIRS], F32, name="pb%d" % t)
            result = keep.tile([P, S], F32, name="result%d" % t)
            for first, count in FIRST_TILE_PIECES if t == 0 else ((0, PAIRS),):
                pairs = slice(first, first + count)
                nc.scalar.activation(minus_pa[:, pairs], s_row[t][:].indirect(entries(n4_t, first, count)), ACT.Copy, scale=-1.0)
                fetch(t == 0 and first == 0, pb[:, pairs], s_row[t], entries(n5_t, first, count))
                nc.vector.tensor_tensor(result[:].indirect(entries(n4_t, first, count)), pb[:, pairs], minus_pa[:, pairs], ALU.add)
            if t == 0:
                rb = keep.tile([P, PAIRS], F32, name="rb")
                nc.vector.scalar_tensor_tensor(rb[:], minus_pa[:], -0.5, pb[:], ALU.mult, ALU.max)
                nc.vector.tensor_copy(result[:].indirect(n5_t[:]), rb[:])
            else:
                turned = psum.tile([P, PAIRS], F32, name="turned%d" % t, tag="d%d" % (2 * t % PACK))
                back = psum.tile([P, PAIRS], F32, name="back%d" % t, tag="d%d" % ((2 * t + 1) % PACK))
                lift_turned = keep.tile([P, PAIRS], F32, name="lift_turned%d" % t)
                lift = keep.tile([P, PAIRS], F32, name="lift%d" % t)
                terms = (pb, pb, minus_pa)
                for b in range(PAIRS // P):
                    block = slice(b * P, (b + 1) * P)
                    for n, term in enumerate(terms):
                        nc.tensor.matmul(turned[:, block], term[:, block], identity[:],
                                         start=n == 0, stop=n == len(terms) - 1, is_transpose=True)
                nc.scalar.activation(lift_turned[:], turned[:], ACT.Relu, scale=-0.5)
                for b in range(PAIRS // P):
                    block = slice(b * P, (b + 1) * P)
                    nc.tensor.transpose(back[:, block], lift_turned[:, block], identity[:])
                nc.scalar.copy(lift[:], back[:])
                nc.vector.tensor_tensor(result[:].indirect(n5_t[:]), pb[:], lift[:], ALU.add)
            nc.sync.dma_start(out_rows[t], result[:])
